import numpy as np
import ml_dtypes


def mxq(x, axis, fmt="e4m3"):
    dtype, down = {"e4m3": (ml_dtypes.float8_e4m3fn, 7), "e5m2": (ml_dtypes.float8_e5m2, 14)}[fmt]
    v = np.moveaxis(np.asarray(x, np.float32).astype(ml_dtypes.bfloat16).astype(np.float64), axis, -1)
    blocks = v.reshape(v.shape[:-1] + (-1, 32))
    amax = np.abs(blocks).max(-1, keepdims=True)
    byte = np.maximum(np.where(amax > 0, np.frexp(amax)[1] - 1 + 127, 0) - down, 1)
    scale = np.exp2(byte - 127.0)
    codes = (blocks / scale).astype(np.float32).astype(dtype).astype(np.float64)
    return np.moveaxis((codes * scale).reshape(v.shape), -1, axis)


WIDE = False


def mx_kscale(k):
    if not WIDE:
        return np.ones(k)
    levels = np.array([10, -10, 5, -5, 0])
    if k % 512:
        return np.exp2(np.random.permutation(np.resize(levels, k // 32))).repeat(32)
    a = np.empty((k // 512, 16))
    for p in range(k // 512):
        a[p, :8] = np.random.permutation(np.resize(levels, 8))
        for g in range(8):
            far = levels[np.abs(levels - a[p, g]) >= 10]
            a[p, g + 8] = far[np.random.randint(len(far))]
    return np.exp2(a.ravel()).repeat(32)


def f64(x):
    return np.asarray(x).astype(np.float64)


def striped(idx):
    return np.tile(idx.reshape(-1, 16).T, (8, 1)).astype(np.uint16)


def unstriped(offs):
    return offs[:16].T.reshape(-1).astype(np.int64)


E2M1 = np.array([0.0, 0.5, 1.0, 1.5, 2.0, 3.0, 4.0, 6.0, -0.0, -0.5, -1.0, -1.5, -2.0, -3.0, -4.0, -6.0])


def pack_weight(w, fmt):
    k, n = w.shape
    w = f64(np.asarray(w, np.float32).astype(ml_dtypes.bfloat16)).reshape(k // 32, 32, n)
    amax = np.abs(w).max(1)
    if fmt == "e4m3":
        byte = np.frexp(amax)[1] - 1 + 127 - 7
    else:
        mant, ex = np.frexp(amax / 6.0)
        byte = np.where(mant > 0.5, ex, ex - 1) + 127
    byte = np.clip(np.where(amax > 0, byte, 1), 1, 254)
    scaled = (w * np.exp2(127.0 - byte)[:, None, :]).reshape(k, n).astype(np.float32)
    by_word = np.ascontiguousarray(scaled.reshape(k // 512, 128, 4, n).transpose(0, 1, 3, 2))
    if fmt == "e4m3":
        words = by_word.astype(ml_dtypes.float8_e4m3fn).view(np.uint8)
    else:
        c = by_word.astype(ml_dtypes.float4_e2m1fn).view(np.uint8) & 0xF
        words = (c[..., 0::2] | (c[..., 1::2] << 4)).reshape(k // 512, 128, 2 * n)
    return np.ascontiguousarray(words), np.ascontiguousarray(byte.astype(np.uint8).reshape(k // 512, 16, n))


def unpack_weight(words, scales, fmt):
    g, _, n = scales.shape
    words = np.ascontiguousarray(words).reshape(g, 128, n, -1)
    if fmt == "e4m3":
        vals = words.view(ml_dtypes.float8_e4m3fn).astype(np.float64)
    else:
        nib = np.empty((g, 128, n, 4), np.uint8)
        nib[..., 0::2] = words & 0xF
        nib[..., 1::2] = words >> 4
        vals = E2M1[nib]
    vals = vals * np.repeat(np.exp2(scales.astype(np.float64) - 127.0), 8, axis=1)[..., None]
    return vals.transpose(0, 1, 3, 2).reshape(g * 512, n)


def gelu(v):
    return 0.5 * v * (1.0 + np.tanh(np.sqrt(2.0 / np.pi) * (v + 0.044715 * v**3)))


K, H, T, S, P, T2 = 1536, 512, 4096, 1024, 1024, 2048

def setup_inputs():
    n = np.random.standard_normal
    s = mx_kscale(K)[:, None]
    u = mx_kscale(H)[:, None]
    d = {}
    d["tab_words"], d["tab_scales"] = pack_weight(n((K, T)) * s, "e4m3")
    d["offs"] = striped(np.random.permutation(T)[:S])
    d["offs2"] = striped(np.random.permutation(T2)[:S])
    d["offs3"] = striped(np.random.permutation(T2)[:P])
    d["offs4"] = striped(np.random.permutation(T2)[:P])
    d["w1"] = (n((K, H)) / s / K**0.5).astype(np.float32)
    d["w2_words"], d["w2_scales"] = pack_weight(n((K, H)) / s * u.T / K**0.5, "e2m1")
    d["wgs"] = np.exp(0.3 * n((128, S))).astype(np.float32)
    d["page0"] = (n((H, T2)) * u).astype(np.float32)
    d["lim"] = (0.5 * n(H) * u[:, 0]).astype(np.float32)
    d["w3"] = (1.5 * n((H, H)) / u / H**0.5).astype(np.float32)
    d["w4_words"], d["w4_scales"] = pack_weight(1.5 * n((H, H)) / u / H**0.5, "e4m3")
    d["gain"] = np.exp(0.3 * n(H)).astype(np.float32)
    d["page1"] = (0.5 * n((H, T2))).astype(np.float32)
    d["wgo"] = np.exp(0.3 * n((128, P))).astype(np.float32)
    return d

def reference(tab_words, tab_scales, offs, offs2, offs3, offs4, w1, w2_words, w2_scales, wgs, page0, lim, w3, w4_words, w4_scales, gain, page1, wgo):
    v = unpack_weight(tab_words, tab_scales, "e4m3")[:, unstriped(offs)]
    a = mxq(f64(w1), 0, "e4m3").T @ v
    b = unpack_weight(w2_words, w2_scales, "e2m1").T @ v
    h = a * b
    page = f64(page0).copy()
    page[:, unstriped(offs2)] = np.tile(f64(wgs), (H // 128, 1)) * h
    x = np.maximum(page[:, unstriped(offs3)], f64(lim)[:, None])
    xq = mxq(x, 0, "e4m3")
    hq = mxq(h, 0, "e4m3")
    e = mxq(f64(w3), 0, "e4m3").T @ xq + unpack_weight(w4_words, w4_scales, "e4m3").T @ hq
    y = 1.0 / (1.0 + np.exp(-f64(gain)[:, None] * (e + a)))
    out = f64(page1).copy()
    out[:, unstriped(offs4)] = np.tile(f64(wgo), (H // 128, 1)) * y
    return out

@@ -1,0 +1,350 @@
+from contextlib import ExitStack
+
+import concourse.mybir as mybir
+from concourse.masks import make_identity
+
+K, H, T, S, T2 = 1536, 512, 4096, 1024, 2048
+FLOPS = 2 * (2 * K * H * S + 2 * H * H * S)
+
+F32 = mybir.dt.float32
+BF16 = mybir.dt.bfloat16
+I32 = mybir.dt.int32
+U32 = mybir.dt.uint32
+U16 = mybir.dt.uint16
+U8 = mybir.dt.uint8
+FP8X4 = mybir.dt.float8_e4m3fn_x4
+FP4X4 = mybir.dt.float4_e2m1fn_x4
+MULT = mybir.AluOpType.mult
+ADD = mybir.AluOpType.add
+SIGMOID = mybir.ActivationFunctionType.Sigmoid
+
+P = 128
+PACK = 4
+K_PASS = P * PACK
+PASSES = K // K_PASS
+QUADS = 4
+QUAD = 32
+HALF = 512
+HALVES = S // HALF
+ALIGN = 64
+LIVE0 = QUAD - 4 * PASSES
+SHIFT_ROWS = QUAD * (QUADS - 1) + 4
+BLOCKS = HALF // P
+CHUNKS = [(0, 0, 256), (0, 256, 256), (1, 0, 512)]
+WEAVE = 256
+
+
+def DIRECT(hf, t):
+    return hf == 0
+
+
+def tile_list_stack_diagnosis_page_kernel(
+    tc, tab_words, tab_scales, offs, offs2, offs3, offs4, w1, w2_words, w2_scales, wgs, page0, lim,
+    w3, w4_words, w4_scales, gain, page1, wgo, out,
+):
+    nc = tc.nc
+    with ExitStack() as ctx:
+        lists = ctx.enter_context(tc.tile_pool(name="lists", bufs=1))
+        sb = ctx.enter_context(tc.tile_pool(name="sb", bufs=1))
+        wide = ctx.enter_context(tc.tile_pool(name="wide", bufs=1))
+        psum = ctx.enter_context(tc.psum_pool(name="psum", bufs=1))
+
+        def tile(shape, dtype, name, tag=None, bufs=1):
+            return sb.tile(shape, dtype, name=name, tag=tag or name, bufs=bufs, align_bytes=ALIGN)
+
+        def load_list(src, name):
+            dst = lists.tile([P, S // 16], U16, name=name)
+            nc.sync.dma_start(dst[:], src)
+            return dst
+
+        def entries(lst, start, count):
+            return lst[:, start // 16 : (start + count) // 16]
+
+        def load_dealt_rows(dst, src, t, cols=slice(0, S)):
+            rows = src.rearrange("(q t) j -> t q j", t=PACK)[t]
+            for c in range(QUADS):
+                nc.sync.dma_start(dst[QUAD * c : QUAD * (c + 1), cols], rows[:, cols])
+
+        def deal_columns(engine_copy, raw, grouped, t0):
+            engine_copy(
+                out=grouped[:].rearrange("p (t m j) -> p m j t", t=2, j=PACK),
+                in_=raw[:].rearrange("p j (m t) -> p m j t", t=PACK)[:, :, :, t0 : t0 + 2],
+            )
+
+        def interleave(dst, src):
+            nc.scalar.copy(
+                out=dst[:].rearrange("p (c i t) -> p c t i", i=4, t=PACK),
+                in_=src[:].rearrange("p t (c i) -> p c t i", i=4),
+            )
+
+        tab_sc = tile([P, T], U8, "tab_sc")
+        w2_sc_raw = tile([P, PASSES, H], U8, "w2_sc_raw")
+        w4_sc = tile([P, H], U8, "w4_sc")
+        picked_sc = [tile([P, S], U8, f"picked_sc{a}") for a in range(PASSES)]
+        nc.vector.memset(w2_sc_raw[:].rearrange("p a c -> p (a c)").bitcast(I32), 0)
+        for q in range(QUADS):
+            nc.vector.memset(tab_sc[QUAD * q : QUAD * q + LIVE0, :].bitcast(I32), 0)
+        for a in range(PASSES):
+            nc.gpsimd.memset(picked_sc[a][:].bitcast(I32), 0)
+        nc.gpsimd.memset(w4_sc[:].bitcast(I32), 0)
+        ident = tile([P, P], F32, "ident")
+        make_identity(nc, ident[:])
+
+        tab_w = [wide.tile([P, T], I32, name=f"tab_w{a}", offset=4 * T * a) for a in range(PASSES)]
+        w1_raw = [tile([P, PACK, H], F32, f"w1_raw{a}", tag=f"raw{a}") for a in range(PASSES)]
+
+        def load_table(a):
+            nc.sync.dma_start(tab_w[a][:], tab_words[a].rearrange("p t i -> p (t i)").bitcast(I32))
+
+        def load_w1(a):
+            nc.sync.dma_start(
+                w1_raw[a][:], w1[a * K_PASS : (a + 1) * K_PASS, :].rearrange("(p j) c -> p j c", j=PACK)
+            )
+
+        idx = load_list(offs, "idx")
+        load_table(0)
+        for q in range(QUADS):
+            nc.scalar.dma_start(
+                tab_sc[QUAD * q + LIVE0 : QUAD * (q + 1), :].bitcast(I32),
+                tab_scales[:, 4 * q : 4 * q + 4, :].bitcast(I32),
+            )
+        w2_raw = tile([P, PASSES, 2 * H], U8, "w2_raw")
+        nc.sync.dma_start(w2_raw[:].bitcast(I32), w2_words.rearrange("a p c -> p a c").bitcast(I32))
+        for q in range(QUADS):
+            nc.sync.dma_start(
+                w2_sc_raw[QUAD * q : QUAD * q + 4, :, :].bitcast(I32),
+                w2_scales[:, 4 * q : 4 * q + 4, :].rearrange("a r c -> r a c").bitcast(I32),
+            )
+        load_table(1)
+        load_w1(0)
+        load_w1(2)
+        load_w1(1)
+        load_table(2)
+        idx2 = load_list(offs2, "idx2")
+        page = [tile([P, T2], F32, f"page{t}") for t in range(PACK)]
+        wgs_sb = [tile([P, S], F32, f"wgs{t}") for t in range(PACK)]
+
+        def load_page(t):
+            nc.sync.dma_start(page[t][:], page0.rearrange("(p t) c -> t p c", t=PACK)[t])
+            if t == 0:
+                for hf in range(HALVES):
+                    load_dealt_rows(wgs_sb[t], wgs, t, slice(hf * HALF, (hf + 1) * HALF))
+            else:
+                load_dealt_rows(wgs_sb[t], wgs, t)
+
+        for t in range(PACK - 1):
+            load_page(t)
+
+        picked_rows = tile([P, S], U8, "picked_rows")
+        nc.vector.tensor_copy(picked_rows[:], tab_sc[:].indirect(idx[:]))
+        for a in range(PASSES):
+            first = LIVE0 + 4 * a
+            nc.scalar.dma_start(
+                picked_sc[a][0:SHIFT_ROWS, :].bitcast(I32),
+                picked_rows[first : first + SHIFT_ROWS, :].bitcast(I32),
+            )
+        picked = [[tile([P, HALF], U32, f"picked{a}_{hf}") for hf in range(HALVES)] for a in range(PASSES)]
+
+        def gather_words(a):
+            for hf in range(HALVES):
+                nc.vector.tensor_copy(
+                    picked[a][hf][:], tab_w[a][:].bitcast(U32).indirect(entries(idx, hf * HALF, HALF))
+                )
+
+        def quantise_w1(a):
+            codes, scales = [], []
+            for g in range(2):
+                grouped = tile([P, 2 * P * PACK], BF16, f"w1_bf{a}_{g}", tag=f"grouped{g}")
+                deal_columns(nc.scalar.copy, w1_raw[a], grouped, 2 * g)
+                cd = tile([P, 2 * P], U32, f"w1_w{a}_{g}")
+                sc = tile([P, 2 * P], U8, f"w1_sc{a}_{g}")
+                nc.vector.quantize_mx(out=cd[:].bitcast(FP8X4), scales=sc[:], in_=grouped[:])
+                codes.append(cd)
+                scales.append(sc)
+            return codes, scales
+
+        gather_words(0)
+        w2_w = tile([P, PASSES, 2 * H], U8, "w2_w")
+        w2_sc = tile([P, PASSES, H], U8, "w2_sc")
+        nc.vector.tensor_copy(
+            out=w2_w[:].bitcast(U16).rearrange("p a (t m) -> p a m t", t=PACK),
+            in_=w2_raw[:].bitcast(U16).rearrange("p a (m t) -> p a m t", t=PACK),
+        )
+        nc.vector.tensor_copy(
+            out=w2_sc[:].rearrange("p a (t m) -> p a m t", t=PACK),
+            in_=w2_sc_raw[:].rearrange("p a (m t) -> p a m t", t=PACK),
+        )
+        gather_words(1)
+        w1_q = {a: quantise_w1(a) for a in (0, 2, 1)}
+        gather_words(2)
+
+        def bank(number, name):
+            return psum.tile([P, HALF], F32, name=name, tag=f"bank{number}")
+
+        idx3 = load_list(offs3, "idx3")
+        idx4 = load_list(offs4, "idx4")
+        lim_sb = tile([P, PACK], F32, "lim_sb")
+        gain_sb = tile([P, PACK], F32, "gain_sb")
+        nc.sync.dma_start(lim_sb[:], lim.rearrange("(p t) -> p t", t=PACK))
+        nc.sync.dma_start(gain_sb[:], gain.rearrange("(p t) -> p t", t=PACK))
+        w3_raw = tile([P, PACK, H], F32, "w3_raw", tag="raw1")
+        nc.sync.dma_start(w3_raw[:], w3.rearrange("(p j) c -> p j c", j=PACK))
+        w4_w = tile([P, H], I32, "w4_w")
+        nc.sync.dma_start(w4_w[:], w4_words[0].rearrange("p c i -> p (c i)").bitcast(I32))
+        for q in range(QUADS):
+            nc.sync.dma_start(
+                w4_sc[QUAD * q : QUAD * q + 4, :].bitcast(I32),
+                w4_scales[0, 4 * q : 4 * q + 4, :].bitcast(I32),
+            )
+        result = [wide.tile([P, T2], F32, name=f"result{t}", offset=4 * T2 * t) for t in range(PACK)]
+        wgo_sb = [wide.tile([P, S], F32, name=f"wgo{t}", offset=4 * (T2 * PACK + S * t)) for t in range(PACK)]
+
+        def load_result(t):
+            nc.sync.dma_start(result[t][:], page1.rearrange("(p t) c -> t p c", t=PACK)[t])
+            load_dealt_rows(wgo_sb[t], wgo, t)
+
+        for t in range(2):
+            load_result(t)
+        load_page(PACK - 1)
+        for t in range(2, PACK):
+            load_result(t)
+
+        bh = [tile([P, PACK, HALF], F32, f"bh{hf}") for hf in range(HALVES)]
+        a_sb = [[tile([P, HALF], F32, f"a_sb{hf}_{t}") for t in range(PACK)] for hf in range(HALVES)]
+        for hf in range(HALVES):
+            cols = slice(hf * HALF, (hf + 1) * HALF)
+            held = []
+            for t in range(PACK):
+                acc = bank(PACK + t, "b_acc")
+                for a in range(PASSES):
+                    nc.tensor.matmul_mx(
+                        out=acc[:],
+                        lhsT=w2_w[:, a, 2 * P * t : 2 * P * (t + 1)].bitcast(FP4X4),
+                        lhsT_scale=w2_sc[:, a, P * t : P * (t + 1)],
+                        rhs=picked[a][hf][:].bitcast(FP8X4),
+                        rhs_scale=picked_sc[a][:, cols],
+                        start=(a == 0),
+                        stop=(a == PASSES - 1),
+                    )
+                nc.scalar.copy(out=bh[hf][:, t, :], in_=acc[:])
+                acc = bank(t, "a_acc")
+                w_cols = slice(P * (t % 2), P * (t % 2 + 1))
+                for a in range(PASSES):
+                    codes, scales = w1_q[a]
+                    nc.tensor.matmul_mx(
+                        out=acc[:],
+                        lhsT=codes[t // 2][:, w_cols].bitcast(FP8X4),
+                        lhsT_scale=scales[t // 2][:, w_cols],
+                        rhs=picked[a][hf][:].bitcast(FP8X4),
+                        rhs_scale=picked_sc[a][:, cols],
+                        start=(a == 0), stop=(a == PASSES - 1),
+                    )
+                if DIRECT(hf, t):
+                    nc.vector.tensor_tensor(bh[hf][:, t, :], acc[:], bh[hf][:, t, :], MULT)
+                    held.append((t, acc))
+                else:
+                    nc.scalar.copy(out=a_sb[hf][t][:], in_=acc[:])
+                    nc.vector.tensor_tensor(bh[hf][:, t, :], a_sb[hf][t][:], bh[hf][:, t, :], MULT)
+                nc.vector.tensor_tensor(
+                    page[t][:].indirect(entries(idx2, hf * HALF, HALF)),
+                    bh[hf][:, t, :], wgs_sb[t][:, cols], MULT,
+                )
+            for t, acc in held:
+                nc.scalar.copy(out=a_sb[hf][t][:], in_=acc[:])
+
+        def quantise_columns(src, width, name, tag):
+            woven = tile([P, width * PACK], BF16, f"{name}_woven", tag=tag)
+            nc.scalar.copy(
+                out=woven[:].rearrange("p (c i t) -> p c t i", i=4, t=PACK),
+                in_=src.rearrange("p t (c i) -> p c t i", i=4),
+            )
+            cd = tile([P, width], U32, f"{name}_w")
+            sc = tile([P, width], U8, f"{name}_sc")
+            nc.vector.quantize_mx(out=cd[:].bitcast(FP8X4), scales=sc[:], in_=woven[:])
+            return cd, sc
+
+        w3_w, w3_sc = quantise_columns(w3_raw[:], H, "w3", "tab_sc")
+
+        a_turned = []
+        for hf in range(HALVES):
+            turned = tile([P, BLOCKS, H], F32, f"a_turned{hf}", tag=f"raw{2 * (1 - hf)}")
+            for blk in range(BLOCKS):
+                acc = bank(PACK + blk, "a_turn")
+                for t in range(PACK):
+                    nc.tensor.transpose(acc[:, P * t : P * (t + 1)], a_sb[hf][t][:, P * blk : P * (blk + 1)], ident[:])
+                nc.scalar.copy(out=turned[:, blk, :], in_=acc[:])
+            a_turned.append(turned)
+        h_q = [quantise_columns(bh[hf][:], HALF, f"h{hf}", f"woven{hf}") for hf in range(HALVES)]
+
+        def recall(hf, recalled):
+            lim_bf = tile([P, PACK, HALF], BF16, f"limited{hf}")
+            for t in range(PACK):
+                got = recalled(t)
+                nc.vector.tensor_copy(got, page[t][:].indirect(entries(idx3, hf * HALF, HALF)))
+                nc.vector.tensor_scalar_max(lim_bf[:, t, :], got, lim_sb[:, t : t + 1])
+            return lim_bf
+
+        def add_turned(sums, src, blk, start, stop):
+            nc.tensor.matmul(
+                sums[:, P * blk : P * (blk + 1)], lhsT=src, rhs=ident[:], is_transpose=True, start=start, stop=stop
+            )
+
+        def e_block(hf, blk, x_q, x0, tag):
+            acc = bank(PACK + blk, "e_acc")
+            h_cols = slice(P * blk, P * (blk + 1))
+            x_cols = slice(P * blk - x0, P * (blk + 1) - x0)
+            nc.tensor.matmul_mx(
+                out=acc[:], lhsT=h_q[hf][0][:, h_cols].bitcast(FP8X4), lhsT_scale=h_q[hf][1][:, h_cols],
+                rhs=w4_w[:].bitcast(FP8X4), rhs_scale=w4_sc[:], start=True, stop=False,
+            )
+            nc.tensor.matmul_mx(
+                out=acc[:], lhsT=x_q[0][:, x_cols].bitcast(FP8X4), lhsT_scale=x_q[1][:, x_cols],
+                rhs=w3_w[:].bitcast(FP8X4), rhs_scale=w3_sc[:], start=False, stop=True,
+            )
+            e_turned = tile([P, H], F32, f"e_turned{hf}_{blk}", tag=tag)
+            nc.scalar.copy(
+                out=e_turned[:].rearrange("p (t m) -> p t m", t=PACK),
+                in_=acc[:].rearrange("p (m t) -> p t m", t=PACK),
+            )
+            return e_turned
+
+        def score(hf, t, sums, e_turned, blocks, y):
+            for blk in blocks:
+                add_turned(sums, a_turned[hf][:, blk, P * t : P * (t + 1)], blk, blk == blocks[0], False)
+            for blk in blocks:
+                add_turned(sums, e_turned[blk][:, P * t : P * (t + 1)], blk, False, blk == blocks[-1])
+            c0, width = P * blocks[0], P * len(blocks)
+            nc.scalar.activation(out=y, in_=sums[:, c0 : c0 + width], func=SIGMOID, scale=gain_sb[:, t : t + 1])
+            start = hf * HALF + c0
+            nc.vector.tensor_tensor(
+                result[t][:].indirect(entries(idx4, start, width)), y, wgo_sb[t][:, start : start + width], MULT
+            )
+
+        recalled0 = tile([P, PACK, HALF], F32, "recalled0", tag="bh0")
+        limited0 = recall(0, lambda t: recalled0[:, t, :])
+        x_q0 = [
+            quantise_columns(limited0[:, :, w0 : w0 + WEAVE], WEAVE, f"x0_{w0}", f"x_woven{w0 // WEAVE}")
+            for w0 in (0, WEAVE)
+        ]
+        tags1 = ["bh1", "x_woven0", "x_woven1", "x_woven0"]
+        limited1 = recall(1, lambda t: tile([P, HALF], F32, f"recalled1_{t}", tag=tags1[t])[:])
+
+        sums = [bank(t, "sums") for t in range(PACK)]
+        y0 = [tile([P, HALF], F32, f"y0_{t}", tag=f"a_sb0_{t}") for t in range(2)]
+        e0 = [e_block(0, 0, x_q0[0], 0, "picked0_0"), e_block(0, 1, x_q0[0], 0, "woven1")]
+        for t in range(2):
+            score(0, t, sums[t], e0, [0, 1], y0[t][:, 0:WEAVE])
+        e0 += [e_block(0, 2, x_q0[1], WEAVE, "picked2_0"), e_block(0, 3, x_q0[1], WEAVE, "picked0_1")]
+        x_q1 = quantise_columns(limited1[:], HALF, "x1", "woven1")
+        for t in range(2):
+            score(0, t, sums[t], e0, [2, 3], y0[t][:, WEAVE:HALF])
+        y0_late = tile([P, 2, HALF], F32, "y0_late", tag="woven1")
+        for t in range(2, PACK):
+            score(0, t, sums[t], e0, [0, 1, 2, 3], y0_late[:, t - 2, :])
+
+        e_tags = ["picked1_1", "picked2_1", "picked0_0", "picked1_0"]
+        e1 = [e_block(1, blk, x_q1, 0, e_tags[blk]) for blk in range(BLOCKS)]
+        for t in range(PACK):
+            y = tile([P, HALF], F32, f"y1_{t}", tag=f"a_sb1_{t}")
+            score(1, t, bank(t, "sums"), e1, [0, 1, 2, 3], y[:])
+            nc.sync.dma_start(out.rearrange("(p t) c -> t p c", t=PACK)[t], result[t][:])

@@ -143,19 +143,19 @@ def tile_list_stack_diagnosis_page_kernel(
                 picked_sc[a][0:SHIFT_ROWS, :].bitcast(I32),
                 picked_rows[first : first + SHIFT_ROWS, :].bitcast(I32),
             )
-        picked = [[tile([P, HALF], U32, f"picked{a}_{hf}") for hf in range(HALVES)] for a in range(PASSES)]
+        picked = [tile([P, S], U32, f"picked{a}") for a in range(PASSES)]
 
         def gather_words(a):
             for hf in range(HALVES):
                 nc.vector.tensor_copy(
-                    picked[a][hf][:], tab_w[a][:].bitcast(U32).indirect(entries(idx, hf * HALF, HALF))
+                    picked[a][:, hf * HALF : (hf + 1) * HALF], tab_w[a][:].bitcast(U32).indirect(entries(idx, hf * HALF, HALF))
                 )
 
         def quantise_w1(a):
             codes, scales = [], []
             for g in range(2):
                 grouped = tile([P, 2 * P * PACK], BF16, f"w1_bf{a}_{g}", tag=f"grouped{g}")
-                deal_columns(nc.scalar.copy, w1_raw[a], grouped, 2 * g)
+                deal_columns((nc.vector.tensor_copy, nc.scalar.copy)[g], w1_raw[a], grouped, 2 * g)
                 cd = tile([P, 2 * P], U32, f"w1_w{a}_{g}")
                 sc = tile([P, 2 * P], U8, f"w1_sc{a}_{g}")
                 nc.vector.quantize_mx(out=cd[:].bitcast(FP8X4), scales=sc[:], in_=grouped[:])
@@ -203,14 +203,13 @@ def tile_list_stack_diagnosis_page_kernel(
             nc.sync.dma_start(result[t][:], page1.rearrange("(p t) c -> t p c", t=PACK)[t])
             load_dealt_rows(wgo_sb[t], wgo, t)
 
-        for t in range(2):
-            load_result(t)
+        load_result(0)
         load_page(PACK - 1)
-        for t in range(2, PACK):
+        for t in range(1, PACK):
             load_result(t)
 
-        bh = [tile([P, PACK, HALF], F32, f"bh{hf}") for hf in range(HALVES)]
-        a_sb = [[tile([P, HALF], F32, f"a_sb{hf}_{t}") for t in range(PACK)] for hf in range(HALVES)]
+        bh = tile([P, PACK, S], F32, "bh")
+        a_sb = [tile([P, S], F32, f"a_sb{t}") for t in range(PACK)]
         for hf in range(HALVES):
             cols = slice(hf * HALF, (hf + 1) * HALF)
             held = []
@@ -221,12 +220,12 @@ def tile_list_stack_diagnosis_page_kernel(
                         out=acc[:],
                         lhsT=w2_w[:, a, 2 * P * t : 2 * P * (t + 1)].bitcast(FP4X4),
                         lhsT_scale=w2_sc[:, a, P * t : P * (t + 1)],
-                        rhs=picked[a][hf][:].bitcast(FP8X4),
+                        rhs=picked[a][:, cols].bitcast(FP8X4),
                         rhs_scale=picked_sc[a][:, cols],
                         start=(a == 0),
                         stop=(a == PASSES - 1),
                     )
-                nc.scalar.copy(out=bh[hf][:, t, :], in_=acc[:])
+                nc.scalar.copy(out=bh[:, t, cols], in_=acc[:])
                 acc = bank(t, "a_acc")
                 w_cols = slice(P * (t % 2), P * (t % 2 + 1))
                 for a in range(PASSES):
@@ -235,35 +234,40 @@ def tile_list_stack_diagnosis_page_kernel(
                         out=acc[:],
                         lhsT=codes[t // 2][:, w_cols].bitcast(FP8X4),
                         lhsT_scale=scales[t // 2][:, w_cols],
-                        rhs=picked[a][hf][:].bitcast(FP8X4),
+                        rhs=picked[a][:, cols].bitcast(FP8X4),
                         rhs_scale=picked_sc[a][:, cols],
                         start=(a == 0), stop=(a == PASSES - 1),
                     )
                 if DIRECT(hf, t):
-                    nc.vector.tensor_tensor(bh[hf][:, t, :], acc[:], bh[hf][:, t, :], MULT)
+                    nc.vector.tensor_tensor(bh[:, t, cols], acc[:], bh[:, t, cols], MULT)
                     held.append((t, acc))
                 else:
-                    nc.scalar.copy(out=a_sb[hf][t][:], in_=acc[:])
-                    nc.vector.tensor_tensor(bh[hf][:, t, :], a_sb[hf][t][:], bh[hf][:, t, :], MULT)
-                nc.vector.tensor_tensor(
-                    page[t][:].indirect(entries(idx2, hf * HALF, HALF)),
-                    bh[hf][:, t, :], wgs_sb[t][:, cols], MULT,
-                )
+                    nc.scalar.copy(out=a_sb[t][:, cols], in_=acc[:])
+                    nc.vector.tensor_tensor(bh[:, t, cols], a_sb[t][:, cols], bh[:, t, cols], MULT)
+                if t == 0:
+                    nc.vector.tensor_tensor(
+                        page[t][:].indirect(entries(idx2, hf * HALF, HALF)),
+                        bh[:, t, cols], wgs_sb[t][:, cols], MULT,
+                    )
+                elif hf == HALVES - 1:
+                    nc.vector.tensor_tensor(page[t][:].indirect(idx2[:]), bh[:, t, :], wgs_sb[t][:], MULT)
             for t, acc in held:
-                nc.scalar.copy(out=a_sb[hf][t][:], in_=acc[:])
+                nc.scalar.copy(out=a_sb[t][:, cols], in_=acc[:])
 
-        def quantise_columns(src, width, name, tag):
+        def quantise_columns(src, width, name, tag, cd=None):
             woven = tile([P, width * PACK], BF16, f"{name}_woven", tag=tag)
             nc.scalar.copy(
                 out=woven[:].rearrange("p (c i t) -> p c t i", i=4, t=PACK),
                 in_=src.rearrange("p t (c i) -> p c t i", i=4),
             )
-            cd = tile([P, width], U32, f"{name}_w")
+            if cd is None:
+                cd = tile([P, width], U32, f"{name}_w")[:]
             sc = tile([P, width], U8, f"{name}_sc")
-            nc.vector.quantize_mx(out=cd[:].bitcast(FP8X4), scales=sc[:], in_=woven[:])
+            nc.vector.quantize_mx(out=cd.bitcast(FP8X4), scales=sc[:], in_=woven[:])
             return cd, sc
 
-        w3_w, w3_sc = quantise_columns(w3_raw[:], H, "w3", "tab_sc")
+        late_w = tile([P, S + H], U32, "late_w", tag="wgs3")
+        w3_w, w3_sc = quantise_columns(w3_raw[:], H, "w3", "tab_sc", late_w[:, S : S + H])
 
         a_turned = []
         for hf in range(HALVES):
@@ -271,10 +275,15 @@ def tile_list_stack_diagnosis_page_kernel(
             for blk in range(BLOCKS):
                 acc = bank(PACK + blk, "a_turn")
                 for t in range(PACK):
-                    nc.tensor.transpose(acc[:, P * t : P * (t + 1)], a_sb[hf][t][:, P * blk : P * (blk + 1)], ident[:])
+                    nc.tensor.transpose(acc[:, P * t : P * (t + 1)], a_sb[t][:, hf * HALF + P * blk : hf * HALF + P * (blk + 1)], ident[:])
                 nc.scalar.copy(out=turned[:, blk, :], in_=acc[:])
             a_turned.append(turned)
-        h_q = [quantise_columns(bh[hf][:], HALF, f"h{hf}", f"woven{hf}") for hf in range(HALVES)]
+        h_q = [
+            quantise_columns(
+                bh[:, :, hf * HALF : (hf + 1) * HALF], HALF, f"h{hf}", ("picked2", "woven1")[hf], late_w[:, hf * HALF : (hf + 1) * HALF]
+            )
+            for hf in range(HALVES)
+        ]
 
         def recall(hf, recalled):
             lim_bf = tile([P, PACK, HALF], BF16, f"limited{hf}")
@@ -299,7 +308,7 @@ def tile_list_stack_diagnosis_page_kernel(
             )
             nc.tensor.matmul_mx(
                 out=acc[:], lhsT=x_q[0][:, x_cols].bitcast(FP8X4), lhsT_scale=x_q[1][:, x_cols],
-                rhs=w3_w[:].bitcast(FP8X4), rhs_scale=w3_sc[:], start=False, stop=True,
+                rhs=w3_w.bitcast(FP8X4), rhs_scale=w3_sc[:], start=False, stop=True,
             )
             e_turned = tile([P, H], F32, f"e_turned{hf}_{blk}", tag=tag)
             nc.scalar.copy(
@@ -308,43 +317,69 @@ def tile_list_stack_diagnosis_page_kernel(
             )
             return e_turned
 
-        def score(hf, t, sums, e_turned, blocks, y):
+        def add_all(hf, t, sums, e_turned, blocks):
             for blk in blocks:
                 add_turned(sums, a_turned[hf][:, blk, P * t : P * (t + 1)], blk, blk == blocks[0], False)
             for blk in blocks:
                 add_turned(sums, e_turned[blk][:, P * t : P * (t + 1)], blk, False, blk == blocks[-1])
+
+        def squash(hf, t, sums, blocks):
             c0, width = P * blocks[0], P * len(blocks)
-            nc.scalar.activation(out=y, in_=sums[:, c0 : c0 + width], func=SIGMOID, scale=gain_sb[:, t : t + 1])
-            start = hf * HALF + c0
-            nc.vector.tensor_tensor(
-                result[t][:].indirect(entries(idx4, start, width)), y, wgo_sb[t][:, start : start + width], MULT
+            nc.scalar.activation(
+                out=y[t][:, hf * HALF + c0 : hf * HALF + c0 + width], in_=sums[:, c0 : c0 + width],
+                func=SIGMOID, scale=gain_sb[:, t : t + 1],
             )
 
-        recalled0 = tile([P, PACK, HALF], F32, "recalled0", tag="bh0")
+        def put(t, start, width):
+            nc.vector.tensor_tensor(
+                result[t][:].indirect(entries(idx4, start, width)),
+                y[t][:, start : start + width], wgo_sb[t][:, start : start + width], MULT,
+            )
+            if start + width == S:
+                nc.sync.dma_start(out.rearrange("(p t) c -> t p c", t=PACK)[t], result[t][:])
+
+        def score(hf, t, sums, e_turned, blocks):
+            add_all(hf, t, sums, e_turned, blocks)
+            squash(hf, t, sums, blocks)
+            if t < PACK - 1:
+                put(t, hf * HALF + P * blocks[0], P * len(blocks))
+
+        recalled0 = tile([P, PACK + 1, HALF], F32, "recalled0", tag="bh")
         limited0 = recall(0, lambda t: recalled0[:, t, :])
         x_q0 = [
             quantise_columns(limited0[:, :, w0 : w0 + WEAVE], WEAVE, f"x0_{w0}", f"x_woven{w0 // WEAVE}")
             for w0 in (0, WEAVE)
         ]
-        tags1 = ["bh1", "x_woven0", "x_woven1", "x_woven0"]
-        limited1 = recall(1, lambda t: tile([P, HALF], F32, f"recalled1_{t}", tag=tags1[t])[:])
+        limited1 = recall(
+            1,
+            lambda t: recalled0[:, PACK, :] if t == 0
+            else tile([P, HALF], F32, f"recalled1_{t}", tag=f"x_woven{(t - 1) % 2}")[:],
+        )
+
+        y = [tile([P, S], F32, f"y{t}", tag=f"a_sb{t}") for t in range(PACK)]
+        sums = [bank(t, "sums") for t in range(PACK)]
+        e0 = [e_block(0, 0, x_q0[0], 0, "picked0"), e_block(0, 1, x_q0[0], 0, "picked1")]
+        for t in range(2):
+            score(0, t, sums[t], e0, [0, 1])
+        e0 += [e_block(0, 2, x_q0[1], WEAVE, "picked2"), e_block(0, 3, x_q0[1], WEAVE, "woven1")]
+        x_q1 = [quantise_columns(limited1[:, :, 0:WEAVE], WEAVE, "x1_0", "picked1")]
+        for t in range(2):
+            score(0, t, sums[t], e0, [2, 3])
+        x_q1.append(None)
+        for t in range(2, PACK):
+            add_all(0, t, sums[t], e0, [0, 1, 2, 3])
+        x_q1[1] = quantise_columns(limited1[:, :, WEAVE:HALF], WEAVE, "x1_1", "woven1")
+        for t in range(2, PACK):
+            squash(0, t, sums[t], [0, 1, 2, 3])
+        put(2, 0, HALF)
 
         sums = [bank(t, "sums") for t in range(PACK)]
-        y0 = [tile([P, HALF], F32, f"y0_{t}", tag=f"a_sb0_{t}") for t in range(2)]
-        e0 = [e_block(0, 0, x_q0[0], 0, "picked0_0"), e_block(0, 1, x_q0[0], 0, "woven1")]
+        e1 = [e_block(1, blk, x_q1[0], 0, f"picked{2 * blk}") for blk in range(2)]
         for t in range(2):
-            score(0, t, sums[t], e0, [0, 1], y0[t][:, 0:WEAVE])
-        e0 += [e_block(0, 2, x_q0[1], WEAVE, "picked2_0"), e_block(0, 3, x_q0[1], WEAVE, "picked0_1")]
-        x_q1 = quantise_columns(limited1[:], HALF, "x1", "woven1")
+            score(1, t, sums[t], e1, [0, 1])
+        e1 += [e_block(1, 2, x_q1[1], WEAVE, "picked1"), e_block(1, 3, x_q1[1], WEAVE, "e_last")]
         for t in range(2):
-            score(0, t, sums[t], e0, [2, 3], y0[t][:, WEAVE:HALF])
-        y0_late = tile([P, 2, HALF], F32, "y0_late", tag="woven1")
+            score(1, t, sums[t], e1, [2, 3])
         for t in range(2, PACK):
-            score(0, t, sums[t], e0, [0, 1, 2, 3], y0_late[:, t - 2, :])
-
-        e_tags = ["picked1_1", "picked2_1", "picked0_0", "picked1_0"]
-        e1 = [e_block(1, blk, x_q1, 0, e_tags[blk]) for blk in range(BLOCKS)]
-        for t in range(PACK):
-            y = tile([P, HALF], F32, f"y1_{t}", tag=f"a_sb1_{t}")
-            score(1, t, bank(t, "sums"), e1, [0, 1, 2, 3], y[:])
-            nc.sync.dma_start(out.rearrange("(p t) c -> t p c", t=PACK)[t], result[t][:])
+            score(1, t, sums[t], e1, [0, 1, 2, 3])
+        put(PACK - 1, 0, S)

@@ -27,8 +27,7 @@ QUAD = 32
 HALF = 512
 HALVES = S // HALF
 ALIGN = 64
-LIVE0 = QUAD - 4 * PASSES
-SHIFT_ROWS = QUAD * (QUADS - 1) + 4
+SHIFT_ROWS = 112
 BLOCKS = HALF // P
 CHUNKS = [(0, 0, 256), (0, 256, 256), (1, 0, 512)]
 WEAVE = 256
@@ -81,12 +80,16 @@ def tile_list_stack_diagnosis_page_kernel(
         w2_sc_raw = tile([P, PASSES, H], U8, "w2_sc_raw")
         w4_sc = tile([P, H], U8, "w4_sc")
         picked_sc = [tile([P, S], U8, f"picked_sc{a}") for a in range(PASSES)]
+        nc.vector.memset(tab_sc[:].bitcast(I32), 0)
         nc.vector.memset(w2_sc_raw[:].rearrange("p a c -> p (a c)").bitcast(I32), 0)
+        nc.vector.memset(w4_sc[:].bitcast(I32), 0)
+        for a in range(1, PASSES):
+            nc.vector.memset(picked_sc[a][:].bitcast(I32), 0)
         for q in range(QUADS):
-            nc.vector.memset(tab_sc[QUAD * q : QUAD * q + LIVE0, :].bitcast(I32), 0)
-        for a in range(PASSES):
-            nc.gpsimd.memset(picked_sc[a][:].bitcast(I32), 0)
-        nc.gpsimd.memset(w4_sc[:].bitcast(I32), 0)
+            nc.gpsimd.dma_start(
+                tab_sc[QUAD * q : QUAD * q + 4 * PASSES, :].bitcast(I32),
+                tab_scales[:, 4 * q : 4 * q + 4, :].bitcast(I32),
+            )
         ident = tile([P, P], F32, "ident")
         make_identity(nc, ident[:])
 
@@ -103,11 +106,6 @@ def tile_list_stack_diagnosis_page_kernel(
 
         idx = load_list(offs, "idx")
         load_table(0)
-        for q in range(QUADS):
-            nc.scalar.dma_start(
-                tab_sc[QUAD * q + LIVE0 : QUAD * (q + 1), :].bitcast(I32),
-                tab_scales[:, 4 * q : 4 * q + 4, :].bitcast(I32),
-            )
         w2_raw = tile([P, PASSES, 2 * H], U8, "w2_raw")
         nc.sync.dma_start(w2_raw[:].bitcast(I32), w2_words.rearrange("a p c -> p a c").bitcast(I32))
         for q in range(QUADS):
@@ -135,13 +133,11 @@ def tile_list_stack_diagnosis_page_kernel(
         for t in range(PACK - 1):
             load_page(t)
 
-        picked_rows = tile([P, S], U8, "picked_rows")
-        nc.vector.tensor_copy(picked_rows[:], tab_sc[:].indirect(idx[:]))
-        for a in range(PASSES):
-            first = LIVE0 + 4 * a
+        nc.vector.tensor_copy(picked_sc[0][:], tab_sc[:].indirect(idx[:]))
+        for a in range(1, PASSES):
             nc.scalar.dma_start(
                 picked_sc[a][0:SHIFT_ROWS, :].bitcast(I32),
-                picked_rows[first : first + SHIFT_ROWS, :].bitcast(I32),
+                picked_sc[0][4 * a : 4 * a + SHIFT_ROWS, :].bitcast(I32),
             )
         picked = [tile([P, S], U32, f"picked{a}") for a in range(PASSES)]
 
@@ -182,11 +178,9 @@ def tile_list_stack_diagnosis_page_kernel(
             return psum.tile([P, HALF], F32, name=name, tag=f"bank{number}")
 
         idx3 = load_list(offs3, "idx3")
-        idx4 = load_list(offs4, "idx4")
         lim_sb = tile([P, PACK], F32, "lim_sb")
         gain_sb = tile([P, PACK], F32, "gain_sb")
         nc.sync.dma_start(lim_sb[:], lim.rearrange("(p t) -> p t", t=PACK))
-        nc.sync.dma_start(gain_sb[:], gain.rearrange("(p t) -> p t", t=PACK))
         w3_raw = tile([P, PACK, H], F32, "w3_raw", tag="raw1")
         nc.sync.dma_start(w3_raw[:], w3.rearrange("(p j) c -> p j c", j=PACK))
         w4_w = tile([P, H], I32, "w4_w")
@@ -205,6 +199,8 @@ def tile_list_stack_diagnosis_page_kernel(
 
         load_result(0)
         load_page(PACK - 1)
+        nc.sync.dma_start(gain_sb[:], gain.rearrange("(p t) -> p t", t=PACK))
+        idx4 = load_list(offs4, "idx4")
         for t in range(1, PACK):
             load_result(t)
 
@@ -266,8 +262,8 @@ def tile_list_stack_diagnosis_page_kernel(
             nc.vector.quantize_mx(out=cd.bitcast(FP8X4), scales=sc[:], in_=woven[:])
             return cd, sc
 
-        late_w = tile([P, S + H], U32, "late_w", tag="wgs3")
-        w3_w, w3_sc = quantise_columns(w3_raw[:], H, "w3", "tab_sc", late_w[:, S : S + H])
+        w3_codes = tile([P, H], U32, "w3_codes", tag="wgs3")
+        w3_w, w3_sc = quantise_columns(w3_raw[:], H, "w3", "tab_sc", w3_codes[:])
 
         a_turned = []
         for hf in range(HALVES):
@@ -278,6 +274,7 @@ def tile_list_stack_diagnosis_page_kernel(
                     nc.tensor.transpose(acc[:, P * t : P * (t + 1)], a_sb[t][:, hf * HALF + P * blk : hf * HALF + P * (blk + 1)], ident[:])
                 nc.scalar.copy(out=turned[:, blk, :], in_=acc[:])
             a_turned.append(turned)
+        late_w = tile([P, S], U32, "late_w", tag="wgs2")
         h_q = [
             quantise_columns(
                 bh[:, :, hf * HALF : (hf + 1) * HALF], HALF, f"h{hf}", ("picked2", "woven1")[hf], late_w[:, hf * HALF : (hf + 1) * HALF]

@@ -15,7 +15,6 @@ U8 = mybir.dt.uint8
 FP8X4 = mybir.dt.float8_e4m3fn_x4
 FP4X4 = mybir.dt.float4_e2m1fn_x4
 MULT = mybir.AluOpType.mult
-ADD = mybir.AluOpType.add
 SIGMOID = mybir.ActivationFunctionType.Sigmoid
 
 P = 128
@@ -29,12 +28,7 @@ HALVES = S // HALF
 ALIGN = 64
 SHIFT_ROWS = 112
 BLOCKS = HALF // P
-CHUNKS = [(0, 0, 256), (0, 256, 256), (1, 0, 512)]
 WEAVE = 256
-
-
-def DIRECT(hf, t):
-    return hf == 0
 
 
 def tile_list_stack_diagnosis_page_kernel(
@@ -59,21 +53,15 @@ def tile_list_stack_diagnosis_page_kernel(
         def entries(lst, start, count):
             return lst[:, start // 16 : (start + count) // 16]
 
-        def load_dealt_rows(dst, src, t, cols=slice(0, S)):
+        def load_dealt_rows(dst, src, t):
             rows = src.rearrange("(q t) j -> t q j", t=PACK)[t]
             for c in range(QUADS):
-                nc.sync.dma_start(dst[QUAD * c : QUAD * (c + 1), cols], rows[:, cols])
+                nc.sync.dma_start(dst[QUAD * c : QUAD * (c + 1), :], rows)
 
         def deal_columns(engine_copy, raw, grouped, t0):
             engine_copy(
                 out=grouped[:].rearrange("p (t m j) -> p m j t", t=2, j=PACK),
                 in_=raw[:].rearrange("p j (m t) -> p m j t", t=PACK)[:, :, :, t0 : t0 + 2],
-            )
-
-        def interleave(dst, src):
-            nc.scalar.copy(
-                out=dst[:].rearrange("p (c i t) -> p c t i", i=4, t=PACK),
-                in_=src[:].rearrange("p t (c i) -> p c t i", i=4),
             )
 
         tab_sc = tile([P, T], U8, "tab_sc")
@@ -114,24 +102,26 @@ def tile_list_stack_diagnosis_page_kernel(
                 w2_scales[:, 4 * q : 4 * q + 4, :].rearrange("a r c -> r a c").bitcast(I32),
             )
         load_table(1)
+        idx2 = load_list(offs2, "idx2")
         load_w1(0)
         load_w1(2)
         load_w1(1)
         load_table(2)
-        idx2 = load_list(offs2, "idx2")
         page = [tile([P, T2], F32, f"page{t}") for t in range(PACK)]
-        wgs_sb = [tile([P, S], F32, f"wgs{t}") for t in range(PACK)]
+        units = [(t, hf) for hf in range(HALVES) for t in range(PACK)]
+        relay = tile([P, (len(units) + 1) * HALF], F32, "relay")
+        h_sb = [relay[:, u * HALF : (u + 1) * HALF] for u in range(len(units))]
+        wgs_sb = [relay[:, (u + 1) * HALF : (u + 2) * HALF] for u in range(len(units))]
 
-        def load_page(t):
+        def load_wgs(u):
+            t, hf = units[u]
+            load_dealt_rows(wgs_sb[u], wgs[:, hf * HALF : (hf + 1) * HALF], t)
+
+        for t in range(PACK):
+            load_wgs(t)
             nc.sync.dma_start(page[t][:], page0.rearrange("(p t) c -> t p c", t=PACK)[t])
-            if t == 0:
-                for hf in range(HALVES):
-                    load_dealt_rows(wgs_sb[t], wgs, t, slice(hf * HALF, (hf + 1) * HALF))
-            else:
-                load_dealt_rows(wgs_sb[t], wgs, t)
-
-        for t in range(PACK - 1):
-            load_page(t)
+        for u in range(PACK, len(units) - 1):
+            load_wgs(u)
 
         nc.vector.tensor_copy(picked_sc[0][:], tab_sc[:].indirect(idx[:]))
         for a in range(1, PASSES):
@@ -198,57 +188,52 @@ def tile_list_stack_diagnosis_page_kernel(
             load_dealt_rows(wgo_sb[t], wgo, t)
 
         load_result(0)
-        load_page(PACK - 1)
+        load_wgs(len(units) - 1)
         nc.sync.dma_start(gain_sb[:], gain.rearrange("(p t) -> p t", t=PACK))
         idx4 = load_list(offs4, "idx4")
         for t in range(1, PACK):
             load_result(t)
 
-        bh = tile([P, PACK, S], F32, "bh")
         a_sb = [tile([P, S], F32, f"a_sb{t}") for t in range(PACK)]
-        for hf in range(HALVES):
+        for u, (t, hf) in enumerate(units):
             cols = slice(hf * HALF, (hf + 1) * HALF)
-            held = []
-            for t in range(PACK):
-                acc = bank(PACK + t, "b_acc")
-                for a in range(PASSES):
-                    nc.tensor.matmul_mx(
-                        out=acc[:],
-                        lhsT=w2_w[:, a, 2 * P * t : 2 * P * (t + 1)].bitcast(FP4X4),
-                        lhsT_scale=w2_sc[:, a, P * t : P * (t + 1)],
-                        rhs=picked[a][:, cols].bitcast(FP8X4),
-                        rhs_scale=picked_sc[a][:, cols],
-                        start=(a == 0),
-                        stop=(a == PASSES - 1),
-                    )
-                nc.scalar.copy(out=bh[:, t, cols], in_=acc[:])
-                acc = bank(t, "a_acc")
-                w_cols = slice(P * (t % 2), P * (t % 2 + 1))
-                for a in range(PASSES):
-                    codes, scales = w1_q[a]
-                    nc.tensor.matmul_mx(
-                        out=acc[:],
-                        lhsT=codes[t // 2][:, w_cols].bitcast(FP8X4),
-                        lhsT_scale=scales[t // 2][:, w_cols],
-                        rhs=picked[a][:, cols].bitcast(FP8X4),
-                        rhs_scale=picked_sc[a][:, cols],
-                        start=(a == 0), stop=(a == PASSES - 1),
-                    )
-                if DIRECT(hf, t):
-                    nc.vector.tensor_tensor(bh[:, t, cols], acc[:], bh[:, t, cols], MULT)
-                    held.append((t, acc))
-                else:
-                    nc.scalar.copy(out=a_sb[t][:, cols], in_=acc[:])
-                    nc.vector.tensor_tensor(bh[:, t, cols], a_sb[t][:, cols], bh[:, t, cols], MULT)
-                if t == 0:
-                    nc.vector.tensor_tensor(
-                        page[t][:].indirect(entries(idx2, hf * HALF, HALF)),
-                        bh[:, t, cols], wgs_sb[t][:, cols], MULT,
-                    )
-                elif hf == HALVES - 1:
-                    nc.vector.tensor_tensor(page[t][:].indirect(idx2[:]), bh[:, t, :], wgs_sb[t][:], MULT)
-            for t, acc in held:
+            acc = bank(PACK + t, "b_acc")
+            for a in range(PASSES):
+                nc.tensor.matmul_mx(
+                    out=acc[:],
+                    lhsT=w2_w[:, a, 2 * P * t : 2 * P * (t + 1)].bitcast(FP4X4),
+                    lhsT_scale=w2_sc[:, a, P * t : P * (t + 1)],
+                    rhs=picked[a][:, cols].bitcast(FP8X4),
+                    rhs_scale=picked_sc[a][:, cols],
+                    start=(a == 0),
+                    stop=(a == PASSES - 1),
+                )
+            b_sb = tile([P, HALF], F32, "b_sb", bufs=len(units))
+            nc.scalar.copy(out=b_sb[:], in_=acc[:])
+            acc = bank(t, "a_acc")
+            w_cols = slice(P * (t % 2), P * (t % 2 + 1))
+            for a in range(PASSES):
+                codes, scales = w1_q[a]
+                nc.tensor.matmul_mx(
+                    out=acc[:],
+                    lhsT=codes[t // 2][:, w_cols].bitcast(FP8X4),
+                    lhsT_scale=scales[t // 2][:, w_cols],
+                    rhs=picked[a][:, cols].bitcast(FP8X4),
+                    rhs_scale=picked_sc[a][:, cols],
+                    start=(a == 0), stop=(a == PASSES - 1),
+                )
+            weighted = tile([P, HALF], F32, "weighted", bufs=3)
+            if u == 0:
+                nc.vector.tensor_tensor(h_sb[u], acc[:], b_sb[:], MULT)
+                nc.vector.tensor_tensor(weighted[:], h_sb[u], wgs_sb[u], MULT)
+                first_acc = acc
+            else:
                 nc.scalar.copy(out=a_sb[t][:, cols], in_=acc[:])
+                nc.gpsimd.tensor_tensor(h_sb[u], a_sb[t][:, cols], b_sb[:], MULT)
+                nc.gpsimd.tensor_tensor(weighted[:], h_sb[u], wgs_sb[u], MULT)
+            if u == 1:
+                nc.scalar.copy(out=a_sb[0][:, 0:HALF], in_=first_acc[:])
+            nc.vector.tensor_copy(page[t][:].indirect(entries(idx2, hf * HALF, HALF)), weighted[:])
 
         def quantise_columns(src, width, name, tag, cd=None):
             woven = tile([P, width * PACK], BF16, f"{name}_woven", tag=tag)
@@ -262,8 +247,8 @@ def tile_list_stack_diagnosis_page_kernel(
             nc.vector.quantize_mx(out=cd.bitcast(FP8X4), scales=sc[:], in_=woven[:])
             return cd, sc
 
-        w3_codes = tile([P, H], U32, "w3_codes", tag="wgs3")
-        w3_w, w3_sc = quantise_columns(w3_raw[:], H, "w3", "tab_sc", w3_codes[:])
+        h_codes = [tile([P, HALF], U32, f"h_codes{hf}", tag="weighted", bufs=3) for hf in range(HALVES)]
+        w3_w, w3_sc = quantise_columns(w3_raw[:], H, "w3", "tab_sc")
 
         a_turned = []
         for hf in range(HALVES):
@@ -274,10 +259,9 @@ def tile_list_stack_diagnosis_page_kernel(
                     nc.tensor.transpose(acc[:, P * t : P * (t + 1)], a_sb[t][:, hf * HALF + P * blk : hf * HALF + P * (blk + 1)], ident[:])
                 nc.scalar.copy(out=turned[:, blk, :], in_=acc[:])
             a_turned.append(turned)
-        late_w = tile([P, S], U32, "late_w", tag="wgs2")
         h_q = [
             quantise_columns(
-                bh[:, :, hf * HALF : (hf + 1) * HALF], HALF, f"h{hf}", ("picked2", "woven1")[hf], late_w[:, hf * HALF : (hf + 1) * HALF]
+                relay[:, hf * PACK * HALF : (hf + 1) * PACK * HALF].rearrange("p (t j) -> p t j", t=PACK), HALF, f"h{hf}", ("picked2", "woven1")[hf], h_codes[hf][:]
             )
             for hf in range(HALVES)
         ]
@@ -341,7 +325,7 @@ def tile_list_stack_diagnosis_page_kernel(
             if t < PACK - 1:
                 put(t, hf * HALF + P * blocks[0], P * len(blocks))
 
-        recalled0 = tile([P, PACK + 1, HALF], F32, "recalled0", tag="bh")
+        recalled0 = tile([P, PACK + 1, HALF], F32, "recalled0", tag="relay")
         limited0 = recall(0, lambda t: recalled0[:, t, :])
         x_q0 = [
             quantise_columns(limited0[:, :, w0 : w0 + WEAVE], WEAVE, f"x0_{w0}", f"x_woven{w0 // WEAVE}")

from contextlib import ExitStack

import concourse.mybir as mybir
from concourse.masks import make_identity

K, H, T, S, T2 = 1536, 512, 4096, 1024, 2048
FLOPS = 2 * (2 * K * H * S + 2 * H * H * S)

F32 = mybir.dt.float32
BF16 = mybir.dt.bfloat16
I32 = mybir.dt.int32
U32 = mybir.dt.uint32
U16 = mybir.dt.uint16
U8 = mybir.dt.uint8
FP8X4 = mybir.dt.float8_e4m3fn_x4
FP4X4 = mybir.dt.float4_e2m1fn_x4
MULT = mybir.AluOpType.mult
SIGMOID = mybir.ActivationFunctionType.Sigmoid

P = 128
PACK = 4
K_PASS = P * PACK
PASSES = K // K_PASS
QUADS = 4
QUAD = 32
HALF = 512
HALVES = S // HALF
ALIGN = 64
SHIFT_ROWS = 112
BLOCKS = HALF // P
WEAVE = 256


def tile_list_stack_diagnosis_page_kernel(
    tc, tab_words, tab_scales, offs, offs2, offs3, offs4, w1, w2_words, w2_scales, wgs, page0, lim,
    w3, w4_words, w4_scales, gain, page1, wgo, out,
):
    nc = tc.nc
    with ExitStack() as ctx:
        lists = ctx.enter_context(tc.tile_pool(name="lists", bufs=1))
        sb = ctx.enter_context(tc.tile_pool(name="sb", bufs=1))
        wide = ctx.enter_context(tc.tile_pool(name="wide", bufs=1))
        psum = ctx.enter_context(tc.psum_pool(name="psum", bufs=1))

        def tile(shape, dtype, name, tag=None, bufs=1):
            return sb.tile(shape, dtype, name=name, tag=tag or name, bufs=bufs, align_bytes=ALIGN)

        def load_list(src, name):
            dst = lists.tile([P, S // 16], U16, name=name)
            nc.sync.dma_start(dst[:], src)
            return dst

        def entries(lst, start, count):
            return lst[:, start // 16 : (start + count) // 16]

        def load_dealt_rows(dst, src, t):
            rows = src.rearrange("(q t) j -> t q j", t=PACK)[t]
            for c in range(QUADS):
                nc.sync.dma_start(dst[QUAD * c : QUAD * (c + 1), :], rows)

        def deal_columns(engine_copy, raw, grouped, t0):
            engine_copy(
                out=grouped[:].rearrange("p (t m j) -> p m j t", t=2, j=PACK),
                in_=raw[:].rearrange("p j (m t) -> p m j t", t=PACK)[:, :, :, t0 : t0 + 2],
            )

        tab_sc = tile([P, T], U8, "tab_sc")
        w2_sc_raw = tile([P, PASSES, H], U8, "w2_sc_raw")
        w4_sc = tile([P, H], U8, "w4_sc")
        picked_sc = [tile([P, S], U8, f"picked_sc{a}") for a in range(PASSES)]
        nc.vector.memset(tab_sc[:].bitcast(I32), 0)
        nc.vector.memset(w2_sc_raw[:].rearrange("p a c -> p (a c)").bitcast(I32), 0)
        nc.vector.memset(w4_sc[:].bitcast(I32), 0)
        for a in range(1, PASSES):
            nc.vector.memset(picked_sc[a][:].bitcast(I32), 0)
        for q in range(QUADS):
            nc.gpsimd.dma_start(
                tab_sc[QUAD * q : QUAD * q + 4 * PASSES, :].bitcast(I32),
                tab_scales[:, 4 * q : 4 * q + 4, :].bitcast(I32),
            )
        ident = tile([P, P], F32, "ident")
        make_identity(nc, ident[:])

        tab_w = [wide.tile([P, T], I32, name=f"tab_w{a}", offset=4 * T * a) for a in range(PASSES)]
        w1_raw = [tile([P, PACK, H], F32, f"w1_raw{a}", tag=f"raw{a}") for a in range(PASSES)]

        def load_table(a):
            nc.sync.dma_start(tab_w[a][:], tab_words[a].rearrange("p t i -> p (t i)").bitcast(I32))

        def load_w1(a):
            nc.sync.dma_start(
                w1_raw[a][:], w1[a * K_PASS : (a + 1) * K_PASS, :].rearrange("(p j) c -> p j c", j=PACK)
            )

        idx = load_list(offs, "idx")
        load_table(0)
        w2_raw = tile([P, PASSES, 2 * H], U8, "w2_raw")
        nc.sync.dma_start(w2_raw[:].bitcast(I32), w2_words.rearrange("a p c -> p a c").bitcast(I32))
        for q in range(QUADS):
            nc.sync.dma_start(
                w2_sc_raw[QUAD * q : QUAD * q + 4, :, :].bitcast(I32),
                w2_scales[:, 4 * q : 4 * q + 4, :].rearrange("a r c -> r a c").bitcast(I32),
            )
        load_table(1)
        idx2 = load_list(offs2, "idx2")
        load_w1(0)
        load_w1(2)
        load_w1(1)
        load_table(2)
        page = [tile([P, T2], F32, f"page{t}") for t in range(PACK)]
        units = [(t, hf) for hf in range(HALVES) for t in range(PACK)]
        relay = tile([P, (len(units) + 1) * HALF], F32, "relay")
        h_sb = [relay[:, u * HALF : (u + 1) * HALF] for u in range(len(units))]
        wgs_sb = [relay[:, (u + 1) * HALF : (u + 2) * HALF] for u in range(len(units))]

        def load_wgs(u):
            t, hf = units[u]
            load_dealt_rows(wgs_sb[u], wgs[:, hf * HALF : (hf + 1) * HALF], t)

        for t in range(PACK):
            load_wgs(t)
            nc.sync.dma_start(page[t][:], page0.rearrange("(p t) c -> t p c", t=PACK)[t])
        for u in range(PACK, len(units) - 1):
            load_wgs(u)

        nc.vector.tensor_copy(picked_sc[0][:], tab_sc[:].indirect(idx[:]))
        for a in range(1, PASSES):
            nc.scalar.dma_start(
                picked_sc[a][0:SHIFT_ROWS, :].bitcast(I32),
                picked_sc[0][4 * a : 4 * a + SHIFT_ROWS, :].bitcast(I32),
            )
        picked = [tile([P, S], U32, f"picked{a}") for a in range(PASSES)]

        def gather_words(a):
            for hf in range(HALVES):
                nc.vector.tensor_copy(
                    picked[a][:, hf * HALF : (hf + 1) * HALF], tab_w[a][:].bitcast(U32).indirect(entries(idx, hf * HALF, HALF))
                )

        def quantise_w1(a):
            codes, scales = [], []
            for g in range(2):
                grouped = tile([P, 2 * P * PACK], BF16, f"w1_bf{a}_{g}", tag=f"grouped{g}")
                deal_columns((nc.vector.tensor_copy, nc.scalar.copy)[g], w1_raw[a], grouped, 2 * g)
                cd = tile([P, 2 * P], U32, f"w1_w{a}_{g}")
                sc = tile([P, 2 * P], U8, f"w1_sc{a}_{g}")
                nc.vector.quantize_mx(out=cd[:].bitcast(FP8X4), scales=sc[:], in_=grouped[:])
                codes.append(cd)
                scales.append(sc)
            return codes, scales

        gather_words(0)
        w2_w = tile([P, PASSES, 2 * H], U8, "w2_w")
        w2_sc = tile([P, PASSES, H], U8, "w2_sc")
        nc.vector.tensor_copy(
            out=w2_w[:].bitcast(U16).rearrange("p a (t m) -> p a m t", t=PACK),
            in_=w2_raw[:].bitcast(U16).rearrange("p a (m t) -> p a m t", t=PACK),
        )
        nc.vector.tensor_copy(
            out=w2_sc[:].rearrange("p a (t m) -> p a m t", t=PACK),
            in_=w2_sc_raw[:].rearrange("p a (m t) -> p a m t", t=PACK),
        )
        gather_words(1)
        w1_q = {a: quantise_w1(a) for a in (0, 2, 1)}
        gather_words(2)

        def bank(number, name):
            return psum.tile([P, HALF], F32, name=name, tag=f"bank{number}")

        idx3 = load_list(offs3, "idx3")
        lim_sb = tile([P, PACK], F32, "lim_sb")
        gain_sb = tile([P, PACK], F32, "gain_sb")
        nc.sync.dma_start(lim_sb[:], lim.rearrange("(p t) -> p t", t=PACK))
        w3_raw = tile([P, PACK, H], F32, "w3_raw", tag="raw1")
        nc.sync.dma_start(w3_raw[:], w3.rearrange("(p j) c -> p j c", j=PACK))
        w4_w = tile([P, H], I32, "w4_w")
        nc.sync.dma_start(w4_w[:], w4_words[0].rearrange("p c i -> p (c i)").bitcast(I32))
        for q in range(QUADS):
            nc.sync.dma_start(
                w4_sc[QUAD * q : QUAD * q + 4, :].bitcast(I32),
                w4_scales[0, 4 * q : 4 * q + 4, :].bitcast(I32),
            )
        result = [wide.tile([P, T2], F32, name=f"result{t}", offset=4 * T2 * t) for t in range(PACK)]
        wgo_sb = [wide.tile([P, S], F32, name=f"wgo{t}", offset=4 * (T2 * PACK + S * t)) for t in range(PACK)]

        def load_result(t):
            nc.sync.dma_start(result[t][:], page1.rearrange("(p t) c -> t p c", t=PACK)[t])
            load_dealt_rows(wgo_sb[t], wgo, t)

        load_result(0)
        load_wgs(len(units) - 1)
        nc.sync.dma_start(gain_sb[:], gain.rearrange("(p t) -> p t", t=PACK))
        idx4 = load_list(offs4, "idx4")
        for t in range(1, PACK):
            load_result(t)

        a_sb = [tile([P, S], F32, f"a_sb{t}") for t in range(PACK)]
        for u, (t, hf) in enumerate(units):
            cols = slice(hf * HALF, (hf + 1) * HALF)
            acc = bank(PACK + t, "b_acc")
            for a in range(PASSES):
                nc.tensor.matmul_mx(
                    out=acc[:],
                    lhsT=w2_w[:, a, 2 * P * t : 2 * P * (t + 1)].bitcast(FP4X4),
                    lhsT_scale=w2_sc[:, a, P * t : P * (t + 1)],
                    rhs=picked[a][:, cols].bitcast(FP8X4),
                    rhs_scale=picked_sc[a][:, cols],
                    start=(a == 0),
                    stop=(a == PASSES - 1),
                )
            b_sb = tile([P, HALF], F32, "b_sb", bufs=len(units))
            nc.scalar.copy(out=b_sb[:], in_=acc[:])
            acc = bank(t, "a_acc")
            w_cols = slice(P * (t % 2), P * (t % 2 + 1))
            for a in range(PASSES):
                codes, scales = w1_q[a]
                nc.tensor.matmul_mx(
                    out=acc[:],
                    lhsT=codes[t // 2][:, w_cols].bitcast(FP8X4),
                    lhsT_scale=scales[t // 2][:, w_cols],
                    rhs=picked[a][:, cols].bitcast(FP8X4),
                    rhs_scale=picked_sc[a][:, cols],
                    start=(a == 0), stop=(a == PASSES - 1),
                )
            weighted = tile([P, HALF], F32, "weighted", bufs=3)
            if u == 0:
                nc.vector.tensor_tensor(h_sb[u], acc[:], b_sb[:], MULT)
                nc.vector.tensor_tensor(weighted[:], h_sb[u], wgs_sb[u], MULT)
                first_acc = acc
            else:
                nc.scalar.copy(out=a_sb[t][:, cols], in_=acc[:])
                nc.gpsimd.tensor_tensor(h_sb[u], a_sb[t][:, cols], b_sb[:], MULT)
                nc.gpsimd.tensor_tensor(weighted[:], h_sb[u], wgs_sb[u], MULT)
            if u == 1:
                nc.scalar.copy(out=a_sb[0][:, 0:HALF], in_=first_acc[:])
            nc.vector.tensor_copy(page[t][:].indirect(entries(idx2, hf * HALF, HALF)), weighted[:])

        def quantise_columns(src, width, name, tag, cd=None):
            woven = tile([P, width * PACK], BF16, f"{name}_woven", tag=tag)
            nc.scalar.copy(
                out=woven[:].rearrange("p (c i t) -> p c t i", i=4, t=PACK),
                in_=src.rearrange("p t (c i) -> p c t i", i=4),
            )
            if cd is None:
                cd = tile([P, width], U32, f"{name}_w")[:]
            sc = tile([P, width], U8, f"{name}_sc")
            nc.vector.quantize_mx(out=cd.bitcast(FP8X4), scales=sc[:], in_=woven[:])
            return cd, sc

        h_codes = [tile([P, HALF], U32, f"h_codes{hf}", tag="weighted", bufs=3) for hf in range(HALVES)]
        w3_w, w3_sc = quantise_columns(w3_raw[:], H, "w3", "tab_sc")

        a_turned = []
        for hf in range(HALVES):
            turned = tile([P, BLOCKS, H], F32, f"a_turned{hf}", tag=f"raw{2 * (1 - hf)}")
            for blk in range(BLOCKS):
                acc = bank(PACK + blk, "a_turn")
                for t in range(PACK):
                    nc.tensor.transpose(acc[:, P * t : P * (t + 1)], a_sb[t][:, hf * HALF + P * blk : hf * HALF + P * (blk + 1)], ident[:])
                nc.scalar.copy(out=turned[:, blk, :], in_=acc[:])
            a_turned.append(turned)
        h_q = [
            quantise_columns(
                relay[:, hf * PACK * HALF : (hf + 1) * PACK * HALF].rearrange("p (t j) -> p t j", t=PACK), HALF, f"h{hf}", ("picked2", "woven1")[hf], h_codes[hf][:]
            )
            for hf in range(HALVES)
        ]

        def recall(hf, recalled):
            lim_bf = tile([P, PACK, HALF], BF16, f"limited{hf}")
            for t in range(PACK):
                got = recalled(t)
                nc.vector.tensor_copy(got, page[t][:].indirect(entries(idx3, hf * HALF, HALF)))
                nc.vector.tensor_scalar_max(lim_bf[:, t, :], got, lim_sb[:, t : t + 1])
            return lim_bf

        def add_turned(sums, src, blk, start, stop):
            nc.tensor.matmul(
                sums[:, P * blk : P * (blk + 1)], lhsT=src, rhs=ident[:], is_transpose=True, start=start, stop=stop
            )

        def e_block(hf, blk, x_q, x0, tag):
            acc = bank(PACK + blk, "e_acc")
            h_cols = slice(P * blk, P * (blk + 1))
            x_cols = slice(P * blk - x0, P * (blk + 1) - x0)
            nc.tensor.matmul_mx(
                out=acc[:], lhsT=h_q[hf][0][:, h_cols].bitcast(FP8X4), lhsT_scale=h_q[hf][1][:, h_cols],
                rhs=w4_w[:].bitcast(FP8X4), rhs_scale=w4_sc[:], start=True, stop=False,
            )
            nc.tensor.matmul_mx(
                out=acc[:], lhsT=x_q[0][:, x_cols].bitcast(FP8X4), lhsT_scale=x_q[1][:, x_cols],
                rhs=w3_w.bitcast(FP8X4), rhs_scale=w3_sc[:], start=False, stop=True,
            )
            e_turned = tile([P, H], F32, f"e_turned{hf}_{blk}", tag=tag)
            nc.scalar.copy(
                out=e_turned[:].rearrange("p (t m) -> p t m", t=PACK),
                in_=acc[:].rearrange("p (m t) -> p t m", t=PACK),
            )
            return e_turned

        def add_all(hf, t, sums, e_turned, blocks):
            for blk in blocks:
                add_turned(sums, a_turned[hf][:, blk, P * t : P * (t + 1)], blk, blk == blocks[0], False)
            for blk in blocks:
                add_turned(sums, e_turned[blk][:, P * t : P * (t + 1)], blk, False, blk == blocks[-1])

        def squash(hf, t, sums, blocks):
            c0, width = P * blocks[0], P * len(blocks)
            nc.scalar.activation(
                out=y[t][:, hf * HALF + c0 : hf * HALF + c0 + width], in_=sums[:, c0 : c0 + width],
                func=SIGMOID, scale=gain_sb[:, t : t + 1],
            )

        def put(t, start, width):
            nc.vector.tensor_tensor(
                result[t][:].indirect(entries(idx4, start, width)),
                y[t][:, start : start + width], wgo_sb[t][:, start : start + width], MULT,
            )
            if start + width == S:
                nc.sync.dma_start(out.rearrange("(p t) c -> t p c", t=PACK)[t], result[t][:])

        def score(hf, t, sums, e_turned, blocks):
            add_all(hf, t, sums, e_turned, blocks)
            squash(hf, t, sums, blocks)
            if t < PACK - 1:
                put(t, hf * HALF + P * blocks[0], P * len(blocks))

        recalled0 = tile([P, PACK + 1, HALF], F32, "recalled0", tag="relay")
        limited0 = recall(0, lambda t: recalled0[:, t, :])
        x_q0 = [
            quantise_columns(limited0[:, :, w0 : w0 + WEAVE], WEAVE, f"x0_{w0}", f"x_woven{w0 // WEAVE}")
            for w0 in (0, WEAVE)
        ]
        limited1 = recall(
            1,
            lambda t: recalled0[:, PACK, :] if t == 0
            else tile([P, HALF], F32, f"recalled1_{t}", tag=f"x_woven{(t - 1) % 2}")[:],
        )

        y = [tile([P, S], F32, f"y{t}", tag=f"a_sb{t}") for t in range(PACK)]
        sums = [bank(t, "sums") for t in range(PACK)]
        e0 = [e_block(0, 0, x_q0[0], 0, "picked0"), e_block(0, 1, x_q0[0], 0, "picked1")]
        for t in range(2):
            score(0, t, sums[t], e0, [0, 1])
        e0 += [e_block(0, 2, x_q0[1], WEAVE, "picked2"), e_block(0, 3, x_q0[1], WEAVE, "woven1")]
        x_q1 = [quantise_columns(limited1[:, :, 0:WEAVE], WEAVE, "x1_0", "picked1")]
        for t in range(2):
            score(0, t, sums[t], e0, [2, 3])
        x_q1.append(None)
        for t in range(2, PACK):
            add_all(0, t, sums[t], e0, [0, 1, 2, 3])
        x_q1[1] = quantise_columns(limited1[:, :, WEAVE:HALF], WEAVE, "x1_1", "woven1")
        for t in range(2, PACK):
            squash(0, t, sums[t], [0, 1, 2, 3])
        put(2, 0, HALF)

        sums = [bank(t, "sums") for t in range(PACK)]
        e1 = [e_block(1, blk, x_q1[0], 0, f"picked{2 * blk}") for blk in range(2)]
        for t in range(2):
            score(1, t, sums[t], e1, [0, 1])
        e1 += [e_block(1, 2, x_q1[1], WEAVE, "picked1"), e_block(1, 3, x_q1[1], WEAVE, "e_last")]
        for t in range(2):
            score(1, t, sums[t], e1, [2, 3])
        for t in range(2, PACK):
            score(1, t, sums[t], e1, [0, 1, 2, 3])
        put(PACK - 1, 0, S)
